import numpy as np
import ml_dtypes


def mxq(x, axis, fmt="e4m3"):
    dtype, down = {"e4m3": (ml_dtypes.float8_e4m3fn, 7), "e5m2": (ml_dtypes.float8_e5m2, 14)}[fmt]
    v = np.moveaxis(np.asarray(x, np.float32).astype(ml_dtypes.bfloat16).astype(np.float64), axis, -1)
    blocks = v.reshape(v.shape[:-1] + (-1, 32))
    amax = np.abs(blocks).max(-1, keepdims=True)
    byte = np.maximum(np.where(amax > 0, np.frexp(amax)[1] - 1 + 127, 0) - down, 1)
    scale = np.exp2(byte - 127.0)
    codes = (blocks / scale).astype(np.float32).astype(dtype).astype(np.float64)
    return np.moveaxis((codes * scale).reshape(v.shape), -1, axis)


WIDE = False


def mx_kscale(k):
    if not WIDE:
        return np.ones(k)
    levels = np.array([10, -10, 5, -5, 0])
    if k % 512:
        return np.exp2(np.random.permutation(np.resize(levels, k // 32))).repeat(32)
    a = np.empty((k // 512, 16))
    for p in range(k // 512):
        a[p, :8] = np.random.permutation(np.resize(levels, 8))
        for g in range(8):
            far = levels[np.abs(levels - a[p, g]) >= 10]
            a[p, g + 8] = far[np.random.randint(len(far))]
    return np.exp2(a.ravel()).repeat(32)


def f64(x):
    return np.asarray(x).astype(np.float64)


def striped(idx):
    return np.tile(idx.reshape(-1, 16).T, (8, 1)).astype(np.uint16)


def unstriped(offs):
    return offs[:16].T.reshape(-1).astype(np.int64)


def striped8(idx):
    return np.concatenate([x.reshape(-1, 16).T for x in idx]).astype(np.uint16)


def runs(offs, k):
    lists = np.stack([offs[16 * r : 16 * r + 16].T.reshape(-1) for r in range(8)]).astype(np.int64)
    return lists[np.arange(k) % 512 // 64]


def pack_weight(w):
    k, n = w.shape
    w = f64(np.asarray(w, np.float32).astype(ml_dtypes.bfloat16)).reshape(k // 32, 32, n)
    amax = np.abs(w).max(1)
    byte = np.clip(np.where(amax > 0, np.frexp(amax)[1] - 1 + 127 - 7, 1), 1, 254)
    scaled = (w * np.exp2(127.0 - byte)[:, None, :]).reshape(k, n).astype(np.float32)
    words = np.ascontiguousarray(scaled.reshape(k // 512, 128, 4, n).transpose(0, 1, 3, 2)).astype(ml_dtypes.float8_e4m3fn).view(np.uint8)
    return words, np.ascontiguousarray(byte.astype(np.uint8).reshape(k // 512, 16, n))


def unpack_weight(words, scales):
    g, p, n, _ = words.shape
    vals = np.ascontiguousarray(words).view(ml_dtypes.float8_e4m3fn).astype(np.float64) * np.repeat(np.exp2(scales.astype(np.float64) - 127.0), 8, axis=1)[..., None]
    return vals.transpose(0, 1, 3, 2).reshape(g * 512, n)


def sigmoid(v):
    return 1.0 / (1.0 + np.exp(-np.maximum(v, -700.0)))


K, T, S, N, H, C = 512, 2048, 512, 512, 512, 512


def setup_inputs():
    n = np.random.standard_normal
    s = mx_kscale(K)[:, None]
    u = mx_kscale(S)
    packed_xT = pack_weight(n((K, T)) * s)
    return {
        "x_words": packed_xT[0],
        "x_scales": packed_xT[1],
        "w1": (n((K, H)) / np.sqrt(K) / s).astype(np.float32),
        "gn": (np.random.uniform(0.5, 1.5, (H, 1)) * u[:, None]).astype(np.float32),
        "w2": (n((H, N)) / np.sqrt(H) / u[:, None]).astype(np.float32),
        "gs": (np.random.uniform(0.5, 1.5, (K, 1)) / s).astype(np.float32),
        "offs": striped(np.random.permutation(T)[:S]),
        "n1": striped8(np.stack([np.random.permutation(S) for _ in range(8)])),
        "n2": striped8(np.stack([np.random.permutation(S) for _ in range(8)])),
        "n3": striped8(np.stack([np.random.permutation(S) for _ in range(8)])),
        "n4": striped8(np.stack([np.random.permutation(S) for _ in range(8)])),
        "n5": striped8(np.stack([np.random.permutation(S) for _ in range(8)])),
        "cand": striped(np.random.permutation(T)[:C]),
        "n6": striped(np.random.permutation(S)),
        "n7": striped(np.random.permutation(S)),
    }


def reference(x_words, x_scales, w1, gn, w2, gs, offs, n1, n2, n3, n4, n5, cand, n6, n7):
    xq = unpack_weight(x_words, x_scales)[:, unstriped(offs)]
    y = mxq(f64(w1), 0, "e4m3").T @ xq
    pa = y[np.arange(H)[:, None], runs(n1, H)]
    z = f64(gn) * (pa + (sigmoid(y[np.arange(H)[:, None], runs(n2, H)])) * (y[np.arange(H)[:, None], runs(n3, H)] - pa))
    a = mxq(f64(w2), 0, "e4m3").T @ mxq(z, 0, "e4m3")
    x_cand = unpack_weight(x_words, x_scales)[:, unstriped(cand)]
    st = y[np.arange(H)[:, None], runs(n4, H)] - y
    z2 = f64(gs) * (y * (sigmoid(st[np.arange(H)[:, None], runs(n5, H)])))
    b = 0.0625 * ((x_cand.T @ mxq(z2, 0, "e4m3")))
    return (a + a[:, unstriped(n6)]) * (sigmoid(b + b[:, unstriped(n7)]))

@@ -1,0 +1,209 @@
+from contextlib import ExitStack
+
+import concourse.mybir as mybir
+
+T, S = 2048, 512
+FLOPS = 3 * 2 * 512 * 512 * 512
+
+F32 = mybir.dt.float32
+BF16 = mybir.dt.bfloat16
+U32 = mybir.dt.uint32
+I32 = mybir.dt.int32
+U16 = mybir.dt.uint16
+U8 = mybir.dt.uint8
+FP8X4 = mybir.dt.float8_e4m3fn_x4
+ALU = mybir.AluOpType
+ACT = mybir.ActivationFunctionType
+
+P = 128
+PACK = 4
+TILES = 4
+HALF = S // 2
+B_FACTOR = 0.0625
+A_FUSED = (1, 2, 3)
+B_FUSED = (3,)
+
+
+def tile_picked_fkcdtrieblerphopd_none_p_kernel(tc, x_words, x_scales, w1, gn, w2, gs, offs, n1, n2, n3, n4, n5, cand, n6, n7, out):
+    nc = tc.nc
+    with ExitStack() as ctx:
+        lists = ctx.enter_context(tc.tile_pool(name="lists", bufs=1))
+        keep = ctx.enter_context(tc.tile_pool(name="keep", bufs=1))
+        psum = ctx.enter_context(tc.psum_pool(name="psum", bufs=1))
+
+        def load_list(name, source):
+            tile = lists.tile([P, S // 16], U16, name=name)
+            nc.sync.dma_start(tile[:], source)
+            return tile
+
+        def rows(name):
+            return [keep.tile([P, S], F32, name="%s%d" % (name, t)) for t in range(TILES)]
+
+        def halves(offsets):
+            return [(slice(h * HALF, (h + 1) * HALF), offsets[:, h * HALF // 16 : (h + 1) * HALF // 16]) for h in range(2)]
+
+        def operand(name):
+            return (keep.tile([P, S], U32, name=name + "_words", align_bytes=64), keep.tile([P, S], U8, name=name + "_scales", align_bytes=64))
+
+        def product(bank, stationary, t, moving, span):
+            cols = slice(t * P, (t + 1) * P)
+            nc.tensor.matmul_mx(
+                out=bank,
+                lhsT=stationary[0][:, cols].bitcast(FP8X4),
+                lhsT_scale=stationary[1][:, cols],
+                rhs=moving[0][:, span].bitcast(FP8X4),
+                rhs_scale=moving[1][:, span],
+                start=True,
+                stop=True,
+            )
+
+        def quantize(packed, grouped, cols):
+            nc.vector.quantize_mx(
+                out=packed[0][:, cols].bitcast(FP8X4),
+                scales=packed[1][:, cols],
+                in_=grouped[:, cols.start * PACK : cols.stop * PACK],
+            )
+
+        table_scales = keep.tile([P, T], U8, name="table_scales")
+        nc.vector.memset(table_scales[:].bitcast(I32), 0)
+        w1_raw = keep.tile([P, PACK, S], F32, name="w1_raw")
+        nc.sync.dma_start(w1_raw[:], w1.rearrange("(p j) c -> p j c", j=PACK))
+        for q in range(4):
+            nc.sync.dma_start(table_scales[32 * q : 32 * q + 4, :].bitcast(I32), x_scales[0, 4 * q : 4 * q + 4, :].bitcast(I32))
+        offs_t = load_list("offs_t", offs)
+        table_words = keep.tile([P, T], U32, name="table_words")
+        nc.sync.dma_start(table_words[:].bitcast(I32), x_words[0].rearrange("p n r -> p (n r)").bitcast(I32))
+        cand_t = load_list("cand_t", cand)
+        n4_t = load_list("n4_t", n4)
+        n1_t = load_list("n1_t", n1)
+        n2_t = load_list("n2_t", n2)
+        n3_t = load_list("n3_t", n3)
+        w2_raw = keep.tile([P, PACK, S], F32, name="w2_raw")
+        nc.sync.dma_start(w2_raw[:], w2.rearrange("(p j) c -> p j c", j=PACK))
+        gn_t = keep.tile([P, PACK], F32, name="gn_t")
+        nc.sync.dma_start(gn_t[:], gn.rearrange("(p t) o -> p (t o)", t=PACK))
+        n5_t = load_list("n5_t", n5)
+        gs_t = keep.tile([P, PACK], F32, name="gs_t")
+        nc.sync.dma_start(gs_t[:], gs.rearrange("(p t) o -> p (t o)", t=PACK))
+        n6_t = load_list("n6_t", n6)
+        n7_t = load_list("n7_t", n7)
+
+        w1_grouped = keep.tile([P, S * PACK], BF16, name="w1_grouped", align_bytes=64)
+        w1_q = operand("w1")
+        picked = operand("picked")
+        cands = operand("cands")
+        dealt_out = w1_grouped[:].rearrange("p (t m j) -> p m j t", t=TILES, j=PACK)
+        dealt_in = w1_raw[:].rearrange("p j (m t) -> p m j t", t=TILES)
+        for u in range(2):
+            nc.scalar.copy(dealt_out[:, :, :, 2 * u : 2 * u + 2], dealt_in[:, :, :, 2 * u : 2 * u + 2])
+        nc.vector.tensor_copy(picked[1][:], table_scales[:].indirect(offs_t[:]))
+        quantize(w1_q, w1_grouped, slice(0, HALF))
+        nc.vector.tensor_copy(picked[0][:], table_words[:].indirect(offs_t[:]))
+        quantize(w1_q, w1_grouped, slice(HALF, S))
+        nc.vector.tensor_copy(cands[1][:], table_scales[:].indirect(cand_t[:]))
+        nc.vector.tensor_copy(cands[0][:], table_words[:].indirect(cand_t[:]))
+
+        y, y_twin = rows("y"), rows("y_twin")
+        pa, s2, dd, mm, st, s5 = rows("pa"), rows("s2"), rows("dd"), rows("mm"), rows("st"), rows("s5")
+        a, a_other, a_sum = rows("a"), rows("a_other"), rows("a_sum")
+        b, b_other, b_sum, gate, res = rows("b"), rows("b_other"), rows("b_sum"), rows("gate"), rows("res")
+        z_rows = keep.tile([P, TILES, S], BF16, name="z_rows")
+        z2_rows = keep.tile([P, TILES, S], BF16, name="z2_rows")
+        w2_grouped = keep.tile([P, S * PACK], BF16, name="w2_grouped", align_bytes=64)
+        z_grouped = keep.tile([P, S * PACK], BF16, name="z_grouped", align_bytes=64)
+        z2_grouped = keep.tile([P, S * PACK], BF16, name="z2_grouped", align_bytes=64)
+        w2_q, z_q, z2_q = operand("w2"), operand("z"), operand("z2")
+        everything = slice(0, S)
+        both = [slice(0, HALF), slice(HALF, S)]
+
+        def interleaved(grouped, planes, cols):
+            return (
+                grouped[:, cols.start * PACK : cols.stop * PACK].rearrange("p (c i t) -> p c t i", i=4, t=PACK),
+                planes[:, :, cols].rearrange("p t (c i) -> p c t i", i=4),
+            )
+
+        def fetch(dst, window, offsets, func):
+            for cols, picks in halves(offsets):
+                nc.scalar.activation(dst[:, cols], window[:].indirect(picks), func)
+
+        def fetch_with(dst, window, offsets, other, op):
+            for cols, picks in halves(offsets):
+                nc.vector.tensor_tensor(dst[:, cols], window[:].indirect(picks), other[:, cols], op)
+
+        def project(t):
+            bank = psum.tile([P, S], F32, name="yb%d" % t)
+            product(bank[:], w1_q, t, picked, everything)
+            nc.scalar.copy(y[t][:], bank[:])
+            nc.sync.dma_start(y_twin[t][:], y[t][:])
+
+        def blend(t):
+            fetch(pa[t], y[t], n1_t, ACT.Copy)
+            if t + 1 < TILES:
+                project(t + 1)
+            fetch(s2[t], y[t], n2_t, ACT.Sigmoid)
+            fetch_with(dd[t], y[t], n3_t, pa[t], ALU.subtract)
+            fetch_with(st[t], y[t], n4_t, y_twin[t], ALU.subtract)
+            nc.vector.scalar_tensor_tensor(mm[t][:], dd[t][:], gn_t[:, t : t + 1], s2[t][:], ALU.mult, ALU.mult)
+            nc.vector.scalar_tensor_tensor(z_rows[:, t, :], pa[t][:], gn_t[:, t : t + 1], mm[t][:], ALU.mult, ALU.add)
+
+        def mix(t):
+            bank = psum.tile([P, S], F32, name="ab%d" % t)
+            product(bank[:], w2_q, t, z_q, everything)
+            nc.scalar.copy(a[t][:], bank[:])
+            if t in A_FUSED:
+                nc.sync.dma_start(a_other[t][:], a[t][:])
+
+        def pair(t):
+            if t in A_FUSED:
+                fetch_with(a_sum[t], a[t], n6_t, a_other[t], ALU.add)
+            else:
+                fetch(a_other[t], a[t], n6_t, ACT.Copy)
+                nc.vector.tensor_tensor(a_sum[t][:], a_other[t][:], a[t][:], ALU.add)
+
+        def leave(t):
+            nc.scalar.activation(b[t][:], b_banks[t][:], ACT.Copy, scale=B_FACTOR)
+            if t in B_FUSED:
+                nc.sync.dma_start(b_other[t][:], b[t][:])
+
+        def judge(t):
+            if t in B_FUSED:
+                fetch_with(b_sum[t], b[t], n7_t, b_other[t], ALU.add)
+            else:
+                fetch(b_other[t], b[t], n7_t, ACT.Copy)
+                nc.vector.tensor_tensor(b_sum[t][:], b_other[t][:], b[t][:], ALU.add)
+
+        def finish(t, cols):
+            nc.scalar.activation(gate[t][:, cols], b_sum[t][:, cols], ACT.Sigmoid)
+            nc.vector.tensor_tensor(res[t][:, cols], a_sum[t][:, cols], gate[t][:, cols], ALU.mult)
+            nc.sync.dma_start(out[t * P : (t + 1) * P, cols], res[t][:, cols])
+
+        project(0)
+        for t in range(TILES):
+            blend(t)
+        nc.scalar.copy(*interleaved(w2_grouped, w2_raw, everything))
+        quantize(w2_q, w2_grouped, everything)
+        nc.vector.tensor_copy(*interleaved(z_grouped, z_rows, both[0]))
+        nc.vector.tensor_copy(*interleaved(z_grouped, z_rows, both[1]))
+        quantize(z_q, z_grouped, everything)
+        for t in range(TILES):
+            mix(t)
+        b_banks = [psum.tile([P, S], F32, name="yb%d" % t) for t in range(TILES)]
+        for cols, picks in halves(n5_t):
+            for t in range(TILES):
+                nc.scalar.activation(s5[t][:, cols], st[t][:].indirect(picks), ACT.Sigmoid)
+                nc.vector.scalar_tensor_tensor(z2_rows[:, t, cols], y[t][:, cols], gs_t[:, t : t + 1], s5[t][:, cols], ALU.mult, ALU.mult)
+            nc.vector.tensor_copy(*interleaved(z2_grouped, z2_rows, cols))
+            quantize(z2_q, z2_grouped, cols)
+            for t in range(TILES):
+                product(b_banks[t][:, cols], cands, t, z2_q, cols)
+        leave(0)
+        leave(TILES - 1)
+        for t in range(TILES):
+            judge(t)
+            if t + 1 < TILES - 1:
+                leave(t + 1)
+            pair(t)
+            if t > 0:
+                finish(t - 1, everything)
+        for cols in both:
+            finish(TILES - 1, cols)

@@ -64,6 +64,11 @@ def tile_picked_fkcdtrieblerphopd_none_p_kernel(tc, x_words, x_scales, w1, gn, w
                 in_=grouped[:, cols.start * PACK : cols.stop * PACK],
             )
 
+        warm_in = keep.tile([P, 1], F32, name="warm_in")
+        warm_out = keep.tile([P, 1], F32, name="warm_out")
+        nc.gpsimd.memset(warm_in[:], 0.0)
+        nc.scalar.activation(warm_out[:], warm_in[:], ACT.Sigmoid)
+
         table_scales = keep.tile([P, T], U8, name="table_scales")
         nc.vector.memset(table_scales[:].bitcast(I32), 0)
         w1_raw = keep.tile([P, PACK, S], F32, name="w1_raw")

@@ -19,9 +19,11 @@ P = 128
 PACK = 4
 TILES = 4
 HALF = S // 2
+WIDE = 1024
+PADDED = 528
 B_FACTOR = 0.0625
-A_FUSED = (1, 2, 3)
-B_FUSED = (3,)
+A_FUSED = (0, 1)
+B_FUSED = (2, 3)
 
 
 def tile_picked_fkcdtrieblerphopd_none_p_kernel(tc, x_words, x_scales, w1, gn, w2, gs, offs, n1, n2, n3, n4, n5, cand, n6, n7, out):
@@ -30,6 +32,9 @@ def tile_picked_fkcdtrieblerphopd_none_p_kernel(tc, x_words, x_scales, w1, gn, w
         lists = ctx.enter_context(tc.tile_pool(name="lists", bufs=1))
         keep = ctx.enter_context(tc.tile_pool(name="keep", bufs=1))
         psum = ctx.enter_context(tc.psum_pool(name="psum", bufs=1))
+        everything = slice(0, S)
+        both = [slice(0, HALF), slice(HALF, S)]
+        spans = [everything]
 
         def load_list(name, source):
             tile = lists.tile([P, S // 16], U16, name=name)
@@ -39,8 +44,14 @@ def tile_picked_fkcdtrieblerphopd_none_p_kernel(tc, x_words, x_scales, w1, gn, w
         def rows(name):
             return [keep.tile([P, S], F32, name="%s%d" % (name, t)) for t in range(TILES)]
 
-        def halves(offsets):
-            return [(slice(h * HALF, (h + 1) * HALF), offsets[:, h * HALF // 16 : (h + 1) * HALF // 16]) for h in range(2)]
+        def windows(name, width):
+            tiles = [keep.tile([P, width], F32, name="%s%d" % (name, t)) for t in range(TILES)]
+            for tile in tiles:
+                nc.vector.memset(tile[:, S:width], 0.0)
+            return tiles
+
+        def entries(offsets, cols):
+            return offsets[:, cols.start // 16 : cols.stop // 16]
 
         def operand(name):
             return (keep.tile([P, S], U32, name=name + "_words", align_bytes=64), keep.tile([P, S], U8, name=name + "_scales", align_bytes=64))
@@ -64,6 +75,20 @@ def tile_picked_fkcdtrieblerphopd_none_p_kernel(tc, x_words, x_scales, w1, gn, w
                 in_=grouped[:, cols.start * PACK : cols.stop * PACK],
             )
 
+        def interleaved(grouped, planes, cols):
+            return (
+                grouped[:, cols.start * PACK : cols.stop * PACK].rearrange("p (c i t) -> p c t i", i=4, t=PACK),
+                planes[:, :, cols].rearrange("p t (c i) -> p c t i", i=4),
+            )
+
+        def fetch(dst, window, offsets, func, spans=spans):
+            for cols in spans:
+                nc.scalar.activation(dst[:, cols], window[:].indirect(entries(offsets, cols)), func)
+
+        def fetch_with(dst, window, offsets, other, op, spans=spans):
+            for cols in spans:
+                nc.vector.tensor_tensor(dst[:, cols], window[:].indirect(entries(offsets, cols)), other[:, cols], op)
+
         warm_in = keep.tile([P, 1], F32, name="warm_in")
         warm_out = keep.tile([P, 1], F32, name="warm_out")
         nc.gpsimd.memset(warm_in[:], 0.0)
@@ -79,10 +104,10 @@ def tile_picked_fkcdtrieblerphopd_none_p_kernel(tc, x_words, x_scales, w1, gn, w
         table_words = keep.tile([P, T], U32, name="table_words")
         nc.sync.dma_start(table_words[:].bitcast(I32), x_words[0].rearrange("p n r -> p (n r)").bitcast(I32))
         cand_t = load_list("cand_t", cand)
-        n4_t = load_list("n4_t", n4)
         n1_t = load_list("n1_t", n1)
-        n2_t = load_list("n2_t", n2)
         n3_t = load_list("n3_t", n3)
+        n2_t = load_list("n2_t", n2)
+        n4_t = load_list("n4_t", n4)
         w2_raw = keep.tile([P, PACK, S], F32, name="w2_raw")
         nc.sync.dma_start(w2_raw[:], w2.rearrange("(p j) c -> p j c", j=PACK))
         gn_t = keep.tile([P, PACK], F32, name="gn_t")
@@ -93,122 +118,140 @@ def tile_picked_fkcdtrieblerphopd_none_p_kernel(tc, x_words, x_scales, w1, gn, w
         n6_t = load_list("n6_t", n6)
         n7_t = load_list("n7_t", n7)
 
+        y, st, a, b = windows("y", WIDE), windows("st", WIDE), windows("a", PADDED), windows("b", PADDED)
+        y_twin, s5 = rows("y_twin"), rows("s5")
+        pa, s2, dd, mm = {}, {}, {}, {}
+        a_other, a_sum = rows("a_other"), rows("a_sum")
+        b_other, b_sum, gate, res = rows("b_other"), rows("b_sum"), rows("gate"), rows("res")
+        z_rows = keep.tile([P, TILES, S], BF16, name="z_rows")
+        z2_rows = keep.tile([P, TILES, S], BF16, name="z2_rows", align_bytes=64)
         w1_grouped = keep.tile([P, S * PACK], BF16, name="w1_grouped", align_bytes=64)
-        w1_q = operand("w1")
-        picked = operand("picked")
-        cands = operand("cands")
+        z_grouped = keep.tile([P, S * PACK], BF16, name="z_grouped", align_bytes=64)
+        z2_grouped = keep.tile([P, S * PACK], BF16, name="z2_grouped", align_bytes=64)
+        w1_q, w2_q, z_q, z2_q = operand("w1"), operand("w2"), operand("z"), operand("z2")
+        picked, cands = operand("picked"), operand("cands")
+
         dealt_out = w1_grouped[:].rearrange("p (t m j) -> p m j t", t=TILES, j=PACK)
         dealt_in = w1_raw[:].rearrange("p j (m t) -> p m j t", t=TILES)
-        for u in range(2):
-            nc.scalar.copy(dealt_out[:, :, :, 2 * u : 2 * u + 2], dealt_in[:, :, :, 2 * u : 2 * u + 2])
+        nc.vector.tensor_copy(dealt_out[:, 80:], dealt_in[:, 80:])
+        nc.scalar.copy(dealt_out[:, :80], dealt_in[:, :80])
         nc.vector.tensor_copy(picked[1][:], table_scales[:].indirect(offs_t[:]))
-        quantize(w1_q, w1_grouped, slice(0, HALF))
-        nc.vector.tensor_copy(picked[0][:], table_words[:].indirect(offs_t[:]))
-        quantize(w1_q, w1_grouped, slice(HALF, S))
+        quantize(w1_q, w1_grouped, everything)
+        for cols in both:
+            nc.vector.tensor_copy(picked[0][:, cols], table_words[:].indirect(entries(offs_t, cols)))
         nc.vector.tensor_copy(cands[1][:], table_scales[:].indirect(cand_t[:]))
         nc.vector.tensor_copy(cands[0][:], table_words[:].indirect(cand_t[:]))
 
-        y, y_twin = rows("y"), rows("y_twin")
-        pa, s2, dd, mm, st, s5 = rows("pa"), rows("s2"), rows("dd"), rows("mm"), rows("st"), rows("s5")
-        a, a_other, a_sum = rows("a"), rows("a_other"), rows("a_sum")
-        b, b_other, b_sum, gate, res = rows("b"), rows("b_other"), rows("b_sum"), rows("gate"), rows("res")
-        z_rows = keep.tile([P, TILES, S], BF16, name="z_rows")
-        z2_rows = keep.tile([P, TILES, S], BF16, name="z2_rows")
-        w2_grouped = keep.tile([P, S * PACK], BF16, name="w2_grouped", align_bytes=64)
-        z_grouped = keep.tile([P, S * PACK], BF16, name="z_grouped", align_bytes=64)
-        z2_grouped = keep.tile([P, S * PACK], BF16, name="z2_grouped", align_bytes=64)
-        w2_q, z_q, z2_q = operand("w2"), operand("z"), operand("z2")
-        everything = slice(0, S)
-        both = [slice(0, HALF), slice(HALF, S)]
+        def project(t, h):
+            bank = psum.tile([P, HALF], F32, name="bank%d" % (2 * t + h))
+            product(bank[:], w1_q, t, picked, both[h])
+            if t == TILES - 1:
+                nc.vector.tensor_copy(y[t][:, both[h]], bank[:])
+            else:
+                nc.scalar.copy(y[t][:, both[h]], bank[:])
+            if h == 1:
+                nc.sync.dma_start(y_twin[t][:], y[t][:, everything])
 
-        def interleaved(grouped, planes, cols):
-            return (
-                grouped[:, cols.start * PACK : cols.stop * PACK].rearrange("p (c i t) -> p c t i", i=4, t=PACK),
-                planes[:, :, cols].rearrange("p t (c i) -> p c t i", i=4),
-            )
+        def scratch(k):
+            return keep.tile([P, S], F32, name="y_twin%d" % k if 0 <= k < TILES else "scratch%d" % (k + 1))
 
-        def fetch(dst, window, offsets, func):
-            for cols, picks in halves(offsets):
-                nc.scalar.activation(dst[:, cols], window[:].indirect(picks), func)
+        def spread(t):
+            pa[t] = keep.tile([P, S], F32, name="pa%d" % (t % 2))
+            dd[t] = scratch(2 * t - 1)
+            fetch(pa[t], y[t], n1_t, ACT.Copy, both if t == 0 else spans)
+            fetch_with(dd[t], y[t], n3_t, pa[t], ALU.subtract, both if t == 0 else spans)
 
-        def fetch_with(dst, window, offsets, other, op):
-            for cols, picks in halves(offsets):
-                nc.vector.tensor_tensor(dst[:, cols], window[:].indirect(picks), other[:, cols], op)
-
-        def project(t):
-            bank = psum.tile([P, S], F32, name="yb%d" % t)
-            product(bank[:], w1_q, t, picked, everything)
-            nc.scalar.copy(y[t][:], bank[:])
-            nc.sync.dma_start(y_twin[t][:], y[t][:])
+        def step(t):
+            fetch_with(st[t], y[t], n4_t, y_twin[t], ALU.subtract)
 
         def blend(t):
-            fetch(pa[t], y[t], n1_t, ACT.Copy)
-            if t + 1 < TILES:
-                project(t + 1)
+            s2[t] = keep.tile([P, S], F32, name="s2%d" % (t % 2))
+            mm[t] = scratch(2 * t)
             fetch(s2[t], y[t], n2_t, ACT.Sigmoid)
-            fetch_with(dd[t], y[t], n3_t, pa[t], ALU.subtract)
-            fetch_with(st[t], y[t], n4_t, y_twin[t], ALU.subtract)
             nc.vector.scalar_tensor_tensor(mm[t][:], dd[t][:], gn_t[:, t : t + 1], s2[t][:], ALU.mult, ALU.mult)
+
+        def gain(t):
             nc.vector.scalar_tensor_tensor(z_rows[:, t, :], pa[t][:], gn_t[:, t : t + 1], mm[t][:], ALU.mult, ALU.add)
 
-        def mix(t):
-            bank = psum.tile([P, S], F32, name="ab%d" % t)
-            product(bank[:], w2_q, t, z_q, everything)
-            nc.scalar.copy(a[t][:], bank[:])
-            if t in A_FUSED:
-                nc.sync.dma_start(a_other[t][:], a[t][:])
+        def weigh(t, cols):
+            nc.vector.scalar_tensor_tensor(z2_rows[:, t, cols], y[t][:, cols], gs_t[:, t : t + 1], s5[t][:, cols], ALU.mult, ALU.mult)
 
-        def pair(t):
+        def leave_a(t):
+            nc.scalar.copy(a[t][:, everything], a_banks[t][:])
             if t in A_FUSED:
-                fetch_with(a_sum[t], a[t], n6_t, a_other[t], ALU.add)
+                nc.scalar.copy(a_other[t][:], a_banks[t][:])
+
+        def pair(t, cols):
+            if t in A_FUSED:
+                fetch_with(a_sum[t], a[t], n6_t, a_other[t], ALU.add, [cols])
             else:
-                fetch(a_other[t], a[t], n6_t, ACT.Copy)
-                nc.vector.tensor_tensor(a_sum[t][:], a_other[t][:], a[t][:], ALU.add)
+                fetch(a_other[t], a[t], n6_t, ACT.Copy, [cols])
+                nc.vector.tensor_tensor(a_sum[t][:, cols], a_other[t][:, cols], a[t][:, cols], ALU.add)
 
-        def leave(t):
-            nc.scalar.activation(b[t][:], b_banks[t][:], ACT.Copy, scale=B_FACTOR)
+        def leave_b(t):
+            nc.scalar.activation(b[t][:, everything], b_banks[t][:], ACT.Copy, scale=B_FACTOR)
             if t in B_FUSED:
-                nc.sync.dma_start(b_other[t][:], b[t][:])
+                nc.sync.dma_start(b_other[t][:], b[t][:, everything])
 
         def judge(t):
             if t in B_FUSED:
                 fetch_with(b_sum[t], b[t], n7_t, b_other[t], ALU.add)
             else:
                 fetch(b_other[t], b[t], n7_t, ACT.Copy)
-                nc.vector.tensor_tensor(b_sum[t][:], b_other[t][:], b[t][:], ALU.add)
+                nc.vector.tensor_tensor(b_sum[t][:], b_other[t][:], b[t][:, everything], ALU.add)
+
+        def squash(t, cols):
+            nc.scalar.activation(gate[t][:, cols], b_sum[t][:, cols], ACT.Sigmoid)
 
         def finish(t, cols):
-            nc.scalar.activation(gate[t][:, cols], b_sum[t][:, cols], ACT.Sigmoid)
             nc.vector.tensor_tensor(res[t][:, cols], a_sum[t][:, cols], gate[t][:, cols], ALU.mult)
             nc.sync.dma_start(out[t * P : (t + 1) * P, cols], res[t][:, cols])
 
-        project(0)
+        project(0, 0)
+        project(1, 0)
+        project(0, 1)
+        spread(0)
+        project(1, 1)
+        for t in range(2, TILES):
+            project(t, 0)
+            project(t, 1)
         for t in range(TILES):
+            step(t)
+            fetch(s5[t], st[t], n5_t, ACT.Sigmoid)
+        blend(0)
+        gain(0)
+        spread(1)
+        blend(1)
+        gain(1)
+        for t in range(TILES):
+            weigh(t, everything)
+        nc.vector.tensor_copy(*interleaved(z2_grouped, z2_rows, everything))
+        quantize(z2_q, z2_grouped, everything)
+        b_banks = [psum.tile([P, S], F32, name="bank%d" % t) for t in range(TILES)]
+        a_banks = [psum.tile([P, S], F32, name="bank%d" % (TILES + t)) for t in range(TILES)]
+        for t in range(2, TILES):
+            spread(t)
             blend(t)
+            gain(t)
+        w2_grouped = keep.tile([P, S * PACK], BF16, name="z2_rows", align_bytes=64)
         nc.scalar.copy(*interleaved(w2_grouped, w2_raw, everything))
         quantize(w2_q, w2_grouped, everything)
-        nc.vector.tensor_copy(*interleaved(z_grouped, z_rows, both[0]))
-        nc.vector.tensor_copy(*interleaved(z_grouped, z_rows, both[1]))
+        nc.vector.tensor_copy(*interleaved(z_grouped, z_rows, everything))
         quantize(z_q, z_grouped, everything)
-        for t in range(TILES):
-            mix(t)
-        b_banks = [psum.tile([P, S], F32, name="yb%d" % t) for t in range(TILES)]
-        for cols, picks in halves(n5_t):
-            for t in range(TILES):
-                nc.scalar.activation(s5[t][:, cols], st[t][:].indirect(picks), ACT.Sigmoid)
-                nc.vector.scalar_tensor_tensor(z2_rows[:, t, cols], y[t][:, cols], gs_t[:, t : t + 1], s5[t][:, cols], ALU.mult, ALU.mult)
-            nc.vector.tensor_copy(*interleaved(z2_grouped, z2_rows, cols))
-            quantize(z2_q, z2_grouped, cols)
-            for t in range(TILES):
-                product(b_banks[t][:, cols], cands, t, z2_q, cols)
-        leave(0)
-        leave(TILES - 1)
+        for t in reversed(range(TILES)):
+            product(b_banks[t][:], cands, t, z2_q, everything)
+            leave_b(t)
         for t in range(TILES):
             judge(t)
-            if t + 1 < TILES - 1:
-                leave(t + 1)
-            pair(t)
-            if t > 0:
-                finish(t - 1, everything)
-        for cols in both:
-            finish(TILES - 1, cols)
+        for t in range(TILES):
+            product(a_banks[t][:], w2_q, t, z_q, everything)
+        gate[2] = keep.tile([P, S], F32, name="z_words", align_bytes=64)
+        gate[3] = keep.tile([P, S], F32, name="w2_words", align_bytes=64)
+        squash(1, everything)
+        for t in range(TILES):
+            leave_a(t)
+            if t != 1:
+                squash(t, everything)
+            for cols in both if t == TILES - 1 else [everything]:
+                pair(t, cols)
+                finish(t, cols)

@@ -3,7 +3,7 @@ from contextlib import ExitStack
 import concourse.mybir as mybir
 
 T, S = 2048, 512
-FLOPS = 3 * 2 * 512 * 512 * 512
+FLOPS = 3 * 2 * S * S * S
 
 F32 = mybir.dt.float32
 BF16 = mybir.dt.bfloat16
@@ -17,11 +17,15 @@ ACT = mybir.ActivationFunctionType
 
 P = 128
 PACK = 4
-TILES = 4
+TILES = S // P
+QUADRANT = 32
+STRIPE = 16
 HALF = S // 2
-WIDE = 1024
-PADDED = 528
+EIGHT_LIST_WINDOW = 2 * S
+ONE_LIST_WINDOW = S + STRIPE
 B_FACTOR = 0.0625
+W1_ON_SCALAR = 80
+EARLY = 2
 A_FUSED = (0, 1)
 B_FUSED = (2, 3)
 
@@ -33,16 +37,18 @@ def tile_picked_fkcdtrieblerphopd_none_p_kernel(tc, x_words, x_scales, w1, gn, w
         keep = ctx.enter_context(tc.tile_pool(name="keep", bufs=1))
         psum = ctx.enter_context(tc.psum_pool(name="psum", bufs=1))
         everything = slice(0, S)
-        both = [slice(0, HALF), slice(HALF, S)]
-        spans = [everything]
+        halves = [slice(0, HALF), slice(HALF, S)]
 
         def load_list(name, source):
-            tile = lists.tile([P, S // 16], U16, name=name)
+            tile = lists.tile([P, S // STRIPE], U16, name=name)
             nc.sync.dma_start(tile[:], source)
             return tile
 
+        def row_tile(name):
+            return keep.tile([P, S], F32, name=name, align_bytes=64)
+
         def rows(name):
-            return [keep.tile([P, S], F32, name="%s%d" % (name, t)) for t in range(TILES)]
+            return [row_tile("%s%d" % (name, t)) for t in range(TILES)]
 
         def windows(name, width):
             tiles = [keep.tile([P, width], F32, name="%s%d" % (name, t)) for t in range(TILES)]
@@ -51,41 +57,39 @@ def tile_picked_fkcdtrieblerphopd_none_p_kernel(tc, x_words, x_scales, w1, gn, w
             return tiles
 
         def entries(offsets, cols):
-            return offsets[:, cols.start // 16 : cols.stop // 16]
+            return offsets[:, cols.start // STRIPE : cols.stop // STRIPE]
 
         def operand(name):
-            return (keep.tile([P, S], U32, name=name + "_words", align_bytes=64), keep.tile([P, S], U8, name=name + "_scales", align_bytes=64))
+            words = keep.tile([P, S], U32, name=name + "_words", align_bytes=64)
+            scales = keep.tile([P, S], U8, name=name + "_scales", align_bytes=64)
+            return words, scales
 
-        def product(bank, stationary, t, moving, span):
-            cols = slice(t * P, (t + 1) * P)
+        def product(bank, stationary, t, moving, cols):
+            tile_cols = slice(t * P, (t + 1) * P)
             nc.tensor.matmul_mx(
                 out=bank,
-                lhsT=stationary[0][:, cols].bitcast(FP8X4),
-                lhsT_scale=stationary[1][:, cols],
-                rhs=moving[0][:, span].bitcast(FP8X4),
-                rhs_scale=moving[1][:, span],
+                lhsT=stationary[0][:, tile_cols].bitcast(FP8X4),
+                lhsT_scale=stationary[1][:, tile_cols],
+                rhs=moving[0][:, cols].bitcast(FP8X4),
+                rhs_scale=moving[1][:, cols],
                 start=True,
                 stop=True,
             )
 
-        def quantize(packed, grouped, cols):
-            nc.vector.quantize_mx(
-                out=packed[0][:, cols].bitcast(FP8X4),
-                scales=packed[1][:, cols],
-                in_=grouped[:, cols.start * PACK : cols.stop * PACK],
-            )
+        def quantize(packed, cols, grouped):
+            nc.vector.quantize_mx(out=packed[0][:, cols].bitcast(FP8X4), scales=packed[1][:, cols], in_=grouped[:])
 
-        def interleaved(grouped, planes, cols):
+        def interleaved(grouped, planes):
             return (
-                grouped[:, cols.start * PACK : cols.stop * PACK].rearrange("p (c i t) -> p c t i", i=4, t=PACK),
-                planes[:, :, cols].rearrange("p t (c i) -> p c t i", i=4),
+                grouped[:].rearrange("p (c i j) -> p c j i", i=4, j=PACK),
+                planes.rearrange("p j (c i) -> p c j i", i=4),
             )
 
-        def fetch(dst, window, offsets, func, spans=spans):
+        def fetch(dst, window, offsets, func, spans):
             for cols in spans:
                 nc.scalar.activation(dst[:, cols], window[:].indirect(entries(offsets, cols)), func)
 
-        def fetch_with(dst, window, offsets, other, op, spans=spans):
+        def fetch_with(dst, window, offsets, other, op, spans):
             for cols in spans:
                 nc.vector.tensor_tensor(dst[:, cols], window[:].indirect(entries(offsets, cols)), other[:, cols], op)
 
@@ -98,8 +102,8 @@ def tile_picked_fkcdtrieblerphopd_none_p_kernel(tc, x_words, x_scales, w1, gn, w
         nc.vector.memset(table_scales[:].bitcast(I32), 0)
         w1_raw = keep.tile([P, PACK, S], F32, name="w1_raw")
         nc.sync.dma_start(w1_raw[:], w1.rearrange("(p j) c -> p j c", j=PACK))
-        for q in range(4):
-            nc.sync.dma_start(table_scales[32 * q : 32 * q + 4, :].bitcast(I32), x_scales[0, 4 * q : 4 * q + 4, :].bitcast(I32))
+        for q in range(P // QUADRANT):
+            nc.sync.dma_start(table_scales[QUADRANT * q : QUADRANT * q + 4, :].bitcast(I32), x_scales[0, 4 * q : 4 * q + 4, :].bitcast(I32))
         offs_t = load_list("offs_t", offs)
         table_words = keep.tile([P, T], U32, name="table_words")
         nc.sync.dma_start(table_words[:].bitcast(I32), x_words[0].rearrange("p n r -> p (n r)").bitcast(I32))
@@ -110,19 +114,21 @@ def tile_picked_fkcdtrieblerphopd_none_p_kernel(tc, x_words, x_scales, w1, gn, w
         n4_t = load_list("n4_t", n4)
         w2_raw = keep.tile([P, PACK, S], F32, name="w2_raw")
         nc.sync.dma_start(w2_raw[:], w2.rearrange("(p j) c -> p j c", j=PACK))
-        gn_t = keep.tile([P, PACK], F32, name="gn_t")
-        nc.sync.dma_start(gn_t[:], gn.rearrange("(p t) o -> p (t o)", t=PACK))
+        gn_t = keep.tile([P, TILES], F32, name="gn_t")
+        nc.sync.dma_start(gn_t[:], gn.rearrange("(p t) o -> p (t o)", t=TILES))
         n5_t = load_list("n5_t", n5)
-        gs_t = keep.tile([P, PACK], F32, name="gs_t")
-        nc.sync.dma_start(gs_t[:], gs.rearrange("(p t) o -> p (t o)", t=PACK))
+        gs_t = keep.tile([P, TILES], F32, name="gs_t")
+        nc.sync.dma_start(gs_t[:], gs.rearrange("(p t) o -> p (t o)", t=TILES))
         n6_t = load_list("n6_t", n6)
         n7_t = load_list("n7_t", n7)
 
-        y, st, a, b = windows("y", WIDE), windows("st", WIDE), windows("a", PADDED), windows("b", PADDED)
+        y, st = windows("y", EIGHT_LIST_WINDOW), windows("st", EIGHT_LIST_WINDOW)
+        a, b = windows("a", ONE_LIST_WINDOW), windows("b", ONE_LIST_WINDOW)
         y_twin, s5 = rows("y_twin"), rows("s5")
         pa, s2, dd, mm = {}, {}, {}, {}
         a_other, a_sum = rows("a_other"), rows("a_sum")
-        b_other, b_sum, gate, res = rows("b_other"), rows("b_sum"), rows("gate"), rows("res")
+        b_other, b_sum = rows("b_other"), rows("b_sum")
+        gate, res = {}, rows("res")
         z_rows = keep.tile([P, TILES, S], BF16, name="z_rows")
         z2_rows = keep.tile([P, TILES, S], BF16, name="z2_rows", align_bytes=64)
         w1_grouped = keep.tile([P, S * PACK], BF16, name="w1_grouped", align_bytes=64)
@@ -133,125 +139,129 @@ def tile_picked_fkcdtrieblerphopd_none_p_kernel(tc, x_words, x_scales, w1, gn, w
 
         dealt_out = w1_grouped[:].rearrange("p (t m j) -> p m j t", t=TILES, j=PACK)
         dealt_in = w1_raw[:].rearrange("p j (m t) -> p m j t", t=TILES)
-        nc.vector.tensor_copy(dealt_out[:, 80:], dealt_in[:, 80:])
-        nc.scalar.copy(dealt_out[:, :80], dealt_in[:, :80])
+        nc.vector.tensor_copy(dealt_out[:, W1_ON_SCALAR:], dealt_in[:, W1_ON_SCALAR:])
+        nc.scalar.copy(dealt_out[:, :W1_ON_SCALAR], dealt_in[:, :W1_ON_SCALAR])
         nc.vector.tensor_copy(picked[1][:], table_scales[:].indirect(offs_t[:]))
-        quantize(w1_q, w1_grouped, everything)
-        for cols in both:
+        quantize(w1_q, everything, w1_grouped)
+        for cols in halves:
             nc.vector.tensor_copy(picked[0][:, cols], table_words[:].indirect(entries(offs_t, cols)))
         nc.vector.tensor_copy(cands[1][:], table_scales[:].indirect(cand_t[:]))
         nc.vector.tensor_copy(cands[0][:], table_words[:].indirect(cand_t[:]))
 
         def project(t, h):
             bank = psum.tile([P, HALF], F32, name="bank%d" % (2 * t + h))
-            product(bank[:], w1_q, t, picked, both[h])
-            if t == TILES - 1:
-                nc.vector.tensor_copy(y[t][:, both[h]], bank[:])
+            product(bank[:], w1_q, t, picked, halves[h])
+            if t < EARLY:
+                nc.scalar.copy(y[t][:, halves[h]], bank[:])
             else:
-                nc.scalar.copy(y[t][:, both[h]], bank[:])
+                nc.vector.tensor_copy(y[t][:, halves[h]], bank[:])
             if h == 1:
                 nc.sync.dma_start(y_twin[t][:], y[t][:, everything])
 
-        def scratch(k):
-            return keep.tile([P, S], F32, name="y_twin%d" % k if 0 <= k < TILES else "scratch%d" % (k + 1))
+        def blend_buffer(k):
+            return row_tile("y_twin%d" % (k - 1) if 1 <= k <= TILES else "blend%d" % k)
+
+        def fetched_buffer(k):
+            return keep.tile([P, S], F32, name="fetched%d" % (k % TILES))
 
         def spread(t):
-            pa[t] = keep.tile([P, S], F32, name="pa%d" % (t % 2))
-            dd[t] = scratch(2 * t - 1)
-            fetch(pa[t], y[t], n1_t, ACT.Copy, both if t == 0 else spans)
-            fetch_with(dd[t], y[t], n3_t, pa[t], ALU.subtract, both if t == 0 else spans)
-
-        def step(t):
-            fetch_with(st[t], y[t], n4_t, y_twin[t], ALU.subtract)
+            spans = halves if t == 0 else [everything]
+            pa[t] = fetched_buffer(t)
+            dd[t] = blend_buffer(2 * t)
+            fetch(pa[t], y[t], n1_t, ACT.Copy, spans)
+            fetch_with(dd[t], y[t], n3_t, pa[t], ALU.subtract, spans)
 
         def blend(t):
-            s2[t] = keep.tile([P, S], F32, name="s2%d" % (t % 2))
-            mm[t] = scratch(2 * t)
-            fetch(s2[t], y[t], n2_t, ACT.Sigmoid)
+            s2[t] = fetched_buffer(t + EARLY)
+            mm[t] = blend_buffer(2 * t + 1)
+            fetch(s2[t], y[t], n2_t, ACT.Sigmoid, [everything])
             nc.vector.scalar_tensor_tensor(mm[t][:], dd[t][:], gn_t[:, t : t + 1], s2[t][:], ALU.mult, ALU.mult)
 
-        def gain(t):
+        def make_z(t):
             nc.vector.scalar_tensor_tensor(z_rows[:, t, :], pa[t][:], gn_t[:, t : t + 1], mm[t][:], ALU.mult, ALU.add)
 
-        def weigh(t, cols):
-            nc.vector.scalar_tensor_tensor(z2_rows[:, t, cols], y[t][:, cols], gs_t[:, t : t + 1], s5[t][:, cols], ALU.mult, ALU.mult)
+        def make_z2(t):
+            nc.vector.scalar_tensor_tensor(z2_rows[:, t, :], y[t][:, everything], gs_t[:, t : t + 1], s5[t][:], ALU.mult, ALU.mult)
 
-        def leave_a(t):
-            nc.scalar.copy(a[t][:, everything], a_banks[t][:])
-            if t in A_FUSED:
-                nc.scalar.copy(a_other[t][:], a_banks[t][:])
+        def sum_b(t):
+            if t in B_FUSED:
+                fetch_with(b_sum[t], b[t], n7_t, b_other[t], ALU.add, [everything])
+            else:
+                fetch(b_other[t], b[t], n7_t, ACT.Copy, [everything])
+                nc.vector.tensor_tensor(b_sum[t][:], b_other[t][:], b[t][:, everything], ALU.add)
 
-        def pair(t, cols):
+        def sum_a(t, cols):
             if t in A_FUSED:
                 fetch_with(a_sum[t], a[t], n6_t, a_other[t], ALU.add, [cols])
             else:
                 fetch(a_other[t], a[t], n6_t, ACT.Copy, [cols])
                 nc.vector.tensor_tensor(a_sum[t][:, cols], a_other[t][:, cols], a[t][:, cols], ALU.add)
 
-        def leave_b(t):
-            nc.scalar.activation(b[t][:, everything], b_banks[t][:], ACT.Copy, scale=B_FACTOR)
-            if t in B_FUSED:
-                nc.sync.dma_start(b_other[t][:], b[t][:, everything])
-
-        def judge(t):
-            if t in B_FUSED:
-                fetch_with(b_sum[t], b[t], n7_t, b_other[t], ALU.add)
-            else:
-                fetch(b_other[t], b[t], n7_t, ACT.Copy)
-                nc.vector.tensor_tensor(b_sum[t][:], b_other[t][:], b[t][:, everything], ALU.add)
-
-        def squash(t, cols):
-            nc.scalar.activation(gate[t][:, cols], b_sum[t][:, cols], ACT.Sigmoid)
-
-        def finish(t, cols):
-            nc.vector.tensor_tensor(res[t][:, cols], a_sum[t][:, cols], gate[t][:, cols], ALU.mult)
-            nc.sync.dma_start(out[t * P : (t + 1) * P, cols], res[t][:, cols])
+        def make_gate(t, buffer_name):
+            gate[t] = row_tile(buffer_name)
+            nc.scalar.activation(gate[t][:], b_sum[t][:], ACT.Sigmoid)
 
         project(0, 0)
         project(1, 0)
         project(0, 1)
         spread(0)
         project(1, 1)
-        for t in range(2, TILES):
+        for t in range(EARLY, TILES):
             project(t, 0)
             project(t, 1)
+
         for t in range(TILES):
-            step(t)
-            fetch(s5[t], st[t], n5_t, ACT.Sigmoid)
+            fetch_with(st[t], y[t], n4_t, y_twin[t], ALU.subtract, [everything])
+            fetch(s5[t], st[t], n5_t, ACT.Sigmoid, [everything])
         blend(0)
-        gain(0)
+        make_z(0)
         spread(1)
         blend(1)
-        gain(1)
+        make_z(1)
         for t in range(TILES):
-            weigh(t, everything)
-        nc.vector.tensor_copy(*interleaved(z2_grouped, z2_rows, everything))
-        quantize(z2_q, z2_grouped, everything)
+            make_z2(t)
+
+        spread(2)
+        nc.vector.tensor_copy(*interleaved(z2_grouped, z2_rows[:]))
+        blend(2)
+        quantize(z2_q, everything, z2_grouped)
+        spread(3)
+        make_z(2)
+        blend(3)
+        make_z(3)
+
         b_banks = [psum.tile([P, S], F32, name="bank%d" % t) for t in range(TILES)]
         a_banks = [psum.tile([P, S], F32, name="bank%d" % (TILES + t)) for t in range(TILES)]
-        for t in range(2, TILES):
-            spread(t)
-            blend(t)
-            gain(t)
-        w2_grouped = keep.tile([P, S * PACK], BF16, name="z2_rows", align_bytes=64)
-        nc.scalar.copy(*interleaved(w2_grouped, w2_raw, everything))
-        quantize(w2_q, w2_grouped, everything)
-        nc.vector.tensor_copy(*interleaved(z_grouped, z_rows, everything))
-        quantize(z_q, z_grouped, everything)
+        w2_grouped = [keep.tile([P, HALF * PACK], BF16, name="s5%d" % (TILES - 2 + h), align_bytes=64) for h in range(2)]
+        for h in range(2):
+            nc.scalar.copy(*interleaved(w2_grouped[h], w2_raw[:, :, halves[h]]))
+        nc.vector.tensor_copy(*interleaved(z_grouped, z_rows[:]))
+        for h in range(2):
+            quantize(w2_q, halves[h], w2_grouped[h])
+        quantize(z_q, everything, z_grouped)
+
         for t in reversed(range(TILES)):
             product(b_banks[t][:], cands, t, z2_q, everything)
-            leave_b(t)
-        for t in range(TILES):
-            judge(t)
+            nc.scalar.activation(b[t][:, everything], b_banks[t][:], ACT.Copy, scale=B_FACTOR)
+            if t in B_FUSED:
+                nc.sync.dma_start(b_other[t][:], b[t][:, everything])
+        for t in (1, 0) + B_FUSED:
+            sum_b(t)
+
         for t in range(TILES):
             product(a_banks[t][:], w2_q, t, z_q, everything)
-        gate[2] = keep.tile([P, S], F32, name="z_words", align_bytes=64)
-        gate[3] = keep.tile([P, S], F32, name="w2_words", align_bytes=64)
-        squash(1, everything)
+        gate_buffers = ["gate0", "gate1", "z_words", "w2_words"]
+        first_gate = 1
+        make_gate(first_gate, gate_buffers[first_gate])
         for t in range(TILES):
-            leave_a(t)
-            if t != 1:
-                squash(t, everything)
-            for cols in both if t == TILES - 1 else [everything]:
-                pair(t, cols)
-                finish(t, cols)
+            nc.scalar.copy(a[t][:, everything], a_banks[t][:])
+            if t in A_FUSED:
+                nc.scalar.copy(a_other[t][:], a_banks[t][:])
+            if t != first_gate:
+                make_gate(t, gate_buffers[t])
+            spans = halves if t == TILES - 1 else [everything]
+            for cols in spans:
+                sum_a(t, cols)
+            for cols in spans:
+                nc.vector.tensor_tensor(res[t][:, cols], a_sum[t][:, cols], gate[t][:, cols], ALU.mult)
+                nc.sync.dma_start(out[t * P : (t + 1) * P, cols], res[t][:, cols])

from contextlib import ExitStack

import concourse.mybir as mybir

T, S = 2048, 512
FLOPS = 3 * 2 * S * S * S

F32 = mybir.dt.float32
BF16 = mybir.dt.bfloat16
U32 = mybir.dt.uint32
I32 = mybir.dt.int32
U16 = mybir.dt.uint16
U8 = mybir.dt.uint8
FP8X4 = mybir.dt.float8_e4m3fn_x4
ALU = mybir.AluOpType
ACT = mybir.ActivationFunctionType

P = 128
PACK = 4
TILES = S // P
QUADRANT = 32
STRIPE = 16
HALF = S // 2
EIGHT_LIST_WINDOW = 2 * S
ONE_LIST_WINDOW = S + STRIPE
B_FACTOR = 0.0625
W1_ON_SCALAR = 80
EARLY = 2
A_FUSED = (0, 1)
B_FUSED = (2, 3)


def tile_picked_fkcdtrieblerphopd_none_p_kernel(tc, x_words, x_scales, w1, gn, w2, gs, offs, n1, n2, n3, n4, n5, cand, n6, n7, out):
    nc = tc.nc
    with ExitStack() as ctx:
        lists = ctx.enter_context(tc.tile_pool(name="lists", bufs=1))
        keep = ctx.enter_context(tc.tile_pool(name="keep", bufs=1))
        psum = ctx.enter_context(tc.psum_pool(name="psum", bufs=1))
        everything = slice(0, S)
        halves = [slice(0, HALF), slice(HALF, S)]

        def load_list(name, source):
            tile = lists.tile([P, S // STRIPE], U16, name=name)
            nc.sync.dma_start(tile[:], source)
            return tile

        def row_tile(name):
            return keep.tile([P, S], F32, name=name, align_bytes=64)

        def rows(name):
            return [row_tile("%s%d" % (name, t)) for t in range(TILES)]

        def windows(name, width):
            tiles = [keep.tile([P, width], F32, name="%s%d" % (name, t)) for t in range(TILES)]
            for tile in tiles:
                nc.vector.memset(tile[:, S:width], 0.0)
            return tiles

        def entries(offsets, cols):
            return offsets[:, cols.start // STRIPE : cols.stop // STRIPE]

        def operand(name):
            words = keep.tile([P, S], U32, name=name + "_words", align_bytes=64)
            scales = keep.tile([P, S], U8, name=name + "_scales", align_bytes=64)
            return words, scales

        def product(bank, stationary, t, moving, cols):
            tile_cols = slice(t * P, (t + 1) * P)
            nc.tensor.matmul_mx(
                out=bank,
                lhsT=stationary[0][:, tile_cols].bitcast(FP8X4),
                lhsT_scale=stationary[1][:, tile_cols],
                rhs=moving[0][:, cols].bitcast(FP8X4),
                rhs_scale=moving[1][:, cols],
                start=True,
                stop=True,
            )

        def quantize(packed, cols, grouped):
            nc.vector.quantize_mx(out=packed[0][:, cols].bitcast(FP8X4), scales=packed[1][:, cols], in_=grouped[:])

        def interleaved(grouped, planes):
            return (
                grouped[:].rearrange("p (c i j) -> p c j i", i=4, j=PACK),
                planes.rearrange("p j (c i) -> p c j i", i=4),
            )

        def fetch(dst, window, offsets, func, spans):
            for cols in spans:
                nc.scalar.activation(dst[:, cols], window[:].indirect(entries(offsets, cols)), func)

        def fetch_with(dst, window, offsets, other, op, spans):
            for cols in spans:
                nc.vector.tensor_tensor(dst[:, cols], window[:].indirect(entries(offsets, cols)), other[:, cols], op)

        warm_in = keep.tile([P, 1], F32, name="warm_in")
        warm_out = keep.tile([P, 1], F32, name="warm_out")
        nc.gpsimd.memset(warm_in[:], 0.0)
        nc.scalar.activation(warm_out[:], warm_in[:], ACT.Sigmoid)

        table_scales = keep.tile([P, T], U8, name="table_scales")
        nc.vector.memset(table_scales[:].bitcast(I32), 0)
        w1_raw = keep.tile([P, PACK, S], F32, name="w1_raw")
        nc.sync.dma_start(w1_raw[:], w1.rearrange("(p j) c -> p j c", j=PACK))
        for q in range(P // QUADRANT):
            nc.sync.dma_start(table_scales[QUADRANT * q : QUADRANT * q + 4, :].bitcast(I32), x_scales[0, 4 * q : 4 * q + 4, :].bitcast(I32))
        offs_t = load_list("offs_t", offs)
        table_words = keep.tile([P, T], U32, name="table_words")
        nc.sync.dma_start(table_words[:].bitcast(I32), x_words[0].rearrange("p n r -> p (n r)").bitcast(I32))
        cand_t = load_list("cand_t", cand)
        n1_t = load_list("n1_t", n1)
        n3_t = load_list("n3_t", n3)
        n2_t = load_list("n2_t", n2)
        n4_t = load_list("n4_t", n4)
        w2_raw = keep.tile([P, PACK, S], F32, name="w2_raw")
        nc.sync.dma_start(w2_raw[:], w2.rearrange("(p j) c -> p j c", j=PACK))
        gn_t = keep.tile([P, TILES], F32, name="gn_t")
        nc.sync.dma_start(gn_t[:], gn.rearrange("(p t) o -> p (t o)", t=TILES))
        n5_t = load_list("n5_t", n5)
        gs_t = keep.tile([P, TILES], F32, name="gs_t")
        nc.sync.dma_start(gs_t[:], gs.rearrange("(p t) o -> p (t o)", t=TILES))
        n6_t = load_list("n6_t", n6)
        n7_t = load_list("n7_t", n7)

        y, st = windows("y", EIGHT_LIST_WINDOW), windows("st", EIGHT_LIST_WINDOW)
        a, b = windows("a", ONE_LIST_WINDOW), windows("b", ONE_LIST_WINDOW)
        y_twin, s5 = rows("y_twin"), rows("s5")
        pa, s2, dd, mm = {}, {}, {}, {}
        a_other, a_sum = rows("a_other"), rows("a_sum")
        b_other, b_sum = rows("b_other"), rows("b_sum")
        gate, res = {}, rows("res")
        z_rows = keep.tile([P, TILES, S], BF16, name="z_rows")
        z2_rows = keep.tile([P, TILES, S], BF16, name="z2_rows", align_bytes=64)
        w1_grouped = keep.tile([P, S * PACK], BF16, name="w1_grouped", align_bytes=64)
        z_grouped = keep.tile([P, S * PACK], BF16, name="z_grouped", align_bytes=64)
        z2_grouped = keep.tile([P, S * PACK], BF16, name="z2_grouped", align_bytes=64)
        w1_q, w2_q, z_q, z2_q = operand("w1"), operand("w2"), operand("z"), operand("z2")
        picked, cands = operand("picked"), operand("cands")

        dealt_out = w1_grouped[:].rearrange("p (t m j) -> p m j t", t=TILES, j=PACK)
        dealt_in = w1_raw[:].rearrange("p j (m t) -> p m j t", t=TILES)
        nc.vector.tensor_copy(dealt_out[:, W1_ON_SCALAR:], dealt_in[:, W1_ON_SCALAR:])
        nc.scalar.copy(dealt_out[:, :W1_ON_SCALAR], dealt_in[:, :W1_ON_SCALAR])
        nc.vector.tensor_copy(picked[1][:], table_scales[:].indirect(offs_t[:]))
        quantize(w1_q, everything, w1_grouped)
        for cols in halves:
            nc.vector.tensor_copy(picked[0][:, cols], table_words[:].indirect(entries(offs_t, cols)))
        nc.vector.tensor_copy(cands[1][:], table_scales[:].indirect(cand_t[:]))
        nc.vector.tensor_copy(cands[0][:], table_words[:].indirect(cand_t[:]))

        def project(t, h):
            bank = psum.tile([P, HALF], F32, name="bank%d" % (2 * t + h))
            product(bank[:], w1_q, t, picked, halves[h])
            if t < EARLY:
                nc.scalar.copy(y[t][:, halves[h]], bank[:])
            else:
                nc.vector.tensor_copy(y[t][:, halves[h]], bank[:])
            if h == 1:
                nc.sync.dma_start(y_twin[t][:], y[t][:, everything])

        def blend_buffer(k):
            return row_tile("y_twin%d" % (k - 1) if 1 <= k <= TILES else "blend%d" % k)

        def fetched_buffer(k):
            return keep.tile([P, S], F32, name="fetched%d" % (k % TILES))

        def spread(t):
            spans = halves if t == 0 else [everything]
            pa[t] = fetched_buffer(t)
            dd[t] = blend_buffer(2 * t)
            fetch(pa[t], y[t], n1_t, ACT.Copy, spans)
            fetch_with(dd[t], y[t], n3_t, pa[t], ALU.subtract, spans)

        def blend(t):
            s2[t] = fetched_buffer(t + EARLY)
            mm[t] = blend_buffer(2 * t + 1)
            fetch(s2[t], y[t], n2_t, ACT.Sigmoid, [everything])
            nc.vector.scalar_tensor_tensor(mm[t][:], dd[t][:], gn_t[:, t : t + 1], s2[t][:], ALU.mult, ALU.mult)

        def make_z(t):
            nc.vector.scalar_tensor_tensor(z_rows[:, t, :], pa[t][:], gn_t[:, t : t + 1], mm[t][:], ALU.mult, ALU.add)

        def make_z2(t):
            nc.vector.scalar_tensor_tensor(z2_rows[:, t, :], y[t][:, everything], gs_t[:, t : t + 1], s5[t][:], ALU.mult, ALU.mult)

        def sum_b(t):
            if t in B_FUSED:
                fetch_with(b_sum[t], b[t], n7_t, b_other[t], ALU.add, [everything])
            else:
                fetch(b_other[t], b[t], n7_t, ACT.Copy, [everything])
                nc.vector.tensor_tensor(b_sum[t][:], b_other[t][:], b[t][:, everything], ALU.add)

        def sum_a(t, cols):
            if t in A_FUSED:
                fetch_with(a_sum[t], a[t], n6_t, a_other[t], ALU.add, [cols])
            else:
                fetch(a_other[t], a[t], n6_t, ACT.Copy, [cols])
                nc.vector.tensor_tensor(a_sum[t][:, cols], a_other[t][:, cols], a[t][:, cols], ALU.add)

        def make_gate(t, buffer_name):
            gate[t] = row_tile(buffer_name)
            nc.scalar.activation(gate[t][:], b_sum[t][:], ACT.Sigmoid)

        project(0, 0)
        project(1, 0)
        project(0, 1)
        spread(0)
        project(1, 1)
        for t in range(EARLY, TILES):
            project(t, 0)
            project(t, 1)

        for t in range(TILES):
            fetch_with(st[t], y[t], n4_t, y_twin[t], ALU.subtract, [everything])
            fetch(s5[t], st[t], n5_t, ACT.Sigmoid, [everything])
        blend(0)
        make_z(0)
        spread(1)
        blend(1)
        make_z(1)
        for t in range(TILES):
            make_z2(t)

        spread(2)
        nc.vector.tensor_copy(*interleaved(z2_grouped, z2_rows[:]))
        blend(2)
        quantize(z2_q, everything, z2_grouped)
        spread(3)
        make_z(2)
        blend(3)
        make_z(3)

        b_banks = [psum.tile([P, S], F32, name="bank%d" % t) for t in range(TILES)]
        a_banks = [psum.tile([P, S], F32, name="bank%d" % (TILES + t)) for t in range(TILES)]
        w2_grouped = [keep.tile([P, HALF * PACK], BF16, name="s5%d" % (TILES - 2 + h), align_bytes=64) for h in range(2)]
        for h in range(2):
            nc.scalar.copy(*interleaved(w2_grouped[h], w2_raw[:, :, halves[h]]))
        nc.vector.tensor_copy(*interleaved(z_grouped, z_rows[:]))
        for h in range(2):
            quantize(w2_q, halves[h], w2_grouped[h])
        quantize(z_q, everything, z_grouped)

        for t in reversed(range(TILES)):
            product(b_banks[t][:], cands, t, z2_q, everything)
            nc.scalar.activation(b[t][:, everything], b_banks[t][:], ACT.Copy, scale=B_FACTOR)
            if t in B_FUSED:
                nc.sync.dma_start(b_other[t][:], b[t][:, everything])
        for t in (1, 0) + B_FUSED:
            sum_b(t)

        for t in range(TILES):
            product(a_banks[t][:], w2_q, t, z_q, everything)
        gate_buffers = ["gate0", "gate1", "z_words", "w2_words"]
        first_gate = 1
        make_gate(first_gate, gate_buffers[first_gate])
        for t in range(TILES):
            nc.scalar.copy(a[t][:, everything], a_banks[t][:])
            if t in A_FUSED:
                nc.scalar.copy(a_other[t][:], a_banks[t][:])
            if t != first_gate:
                make_gate(t, gate_buffers[t])
            spans = halves if t == TILES - 1 else [everything]
            for cols in spans:
                sum_a(t, cols)
            for cols in spans:
                nc.vector.tensor_tensor(res[t][:, cols], a_sum[t][:, cols], gate[t][:, cols], ALU.mult)
                nc.sync.dma_start(out[t * P : (t + 1) * P, cols], res[t][:, cols])
